import numpy as np
import ml_dtypes

BF16 = ml_dtypes.bfloat16


def bf(x):
    return np.asarray(x, np.float32).astype(BF16)


def f32(x):
    return np.asarray(x, np.float32)


def f64(x):
    return np.asarray(x).astype(np.float64)


def striped(idx):
    return np.concatenate([l.reshape(-1, 16).T for l in idx])


def rows(idx, k):
    return np.tile(np.repeat(idx, 16, axis=0), (k // (16 * 8), 1))


def look(tab, idx):
    return np.take_along_axis(f64(tab), rows(idx, len(tab)), axis=1)


K, S, V, N, M = 256, 2048, 512, 512, 512


def setup_inputs():
    return {"tab": f32(np.random.standard_normal((2, K, S))), "w": bf(np.random.standard_normal((K, M)) / np.sqrt(K)), "b": f32(0.5 * np.random.standard_normal((M, 1))), "offs": striped(np.stack([np.random.permutation(S)[:N] for _ in range(8)]))}


def reference(tab, w, b, offs):
    idx = np.stack([g.T.reshape(-1) for g in np.split(offs, 8)])
    x = (look(tab[0], idx) - 0.125) * 1.5 / (1.0 + np.exp(-look(tab[1], idx)))
    return np.maximum(f64(w).T @ x + f64(b), 0.0)

@@ -1,0 +1,66 @@
+import concourse.mybir as mybir
+
+P = 128
+F32 = mybir.dt.float32
+BF16 = mybir.dt.bfloat16
+U16 = mybir.dt.uint16
+ALU = mybir.AluOpType
+ACT = mybir.ActivationFunctionType
+
+FLOPS = 2 * 256 * 512 * 512
+
+
+def tile_lookup_gnorm_relu_kernel(tc, tab, w, b, offs, out):
+    nc = tc.nc
+    rows, places = tab.shape[1], tab.shape[2]
+    features = w.shape[1]
+    n = offs.shape[1] * 16
+    row_blocks = rows // P
+    feature_blocks = features // P
+
+    with (
+        tc.tile_pool(name="held", bufs=1) as held,
+        tc.psum_pool(name="psum", bufs=1) as psum,
+    ):
+        lists = held.tile([P, n // 16], U16, name="lists")
+        nc.sync.dma_start(lists[:], offs)
+
+        bias = held.tile([P, feature_blocks], F32, name="bias")
+        with nc.allow_non_contiguous_dma(reason="512 bias values, one to a partition and block"):
+            nc.scalar.dma_start(bias[:], b.rearrange("(c p) o -> p (c o)", p=P))
+
+        gate_windows = [held.tile([P, places], F32, name=f"gates{k}") for k in range(row_blocks)]
+        value_windows = [held.tile([P, places], F32, name=f"values{k}") for k in range(row_blocks)]
+        weights = held.tile([P, row_blocks, features], BF16, name="weights")
+        for k in range(row_blocks):
+            block = slice(k * P, (k + 1) * P)
+            nc.sync.dma_start(gate_windows[k][:], tab[1, block, :])
+            nc.sync.dma_start(value_windows[k][:], tab[0, block, :])
+            nc.sync.dma_start(weights[:, k, :], w[block, :])
+
+        sums = [psum.tile([P, n], F32, name=f"sums{c}") for c in range(feature_blocks)]
+        for k in range(row_blocks):
+            gates = held.tile([P, n], F32, name=f"picked_gates{k}")
+            nc.scalar.activation(gates[:], gate_windows[k][:].indirect(lists[:]), ACT.Sigmoid)
+            values = held.tile([P, n], F32, name=f"picked_values{k}")
+            nc.vector.tensor_scalar(
+                values[:], value_windows[k][:].indirect(lists[:]), 0.125, 1.5, ALU.subtract, ALU.mult
+            )
+            x = held.tile([P, n], BF16, name=f"x{k}")
+            nc.vector.tensor_tensor(x[:], values[:], gates[:], ALU.mult)
+            for c in range(feature_blocks):
+                nc.tensor.matmul(
+                    sums[c][:],
+                    weights[:, k, c * P : (c + 1) * P],
+                    x[:],
+                    start=(k == 0),
+                    stop=(k == row_blocks - 1),
+                )
+
+        for c in range(feature_blocks):
+            result = held.tile([P, n], F32, name=f"result{c}")
+            if c % 2 == 0:
+                nc.scalar.activation(result[:], sums[c][:], ACT.Relu, bias=bias[:, c : c + 1])
+            else:
+                nc.vector.tensor_scalar(result[:], sums[c][:], bias[:, c : c + 1], 0.0, ALU.add, ALU.max)
+            nc.sync.dma_start(out[c * P : (c + 1) * P, :], result[:])

@@ -8,6 +8,8 @@ ALU = mybir.AluOpType
 ACT = mybir.ActivationFunctionType
 
 FLOPS = 2 * 256 * 512 * 512
+HALVES = 2
+WARM_UPS = 10
 
 
 def tile_lookup_gnorm_relu_kernel(tc, tab, w, b, offs, out):
@@ -16,7 +18,8 @@ def tile_lookup_gnorm_relu_kernel(tc, tab, w, b, offs, out):
     features = w.shape[1]
     n = offs.shape[1] * 16
     row_blocks = rows // P
-    feature_blocks = features // P
+    per_partition = features // P
+    half = n // HALVES
 
     with (
         tc.tile_pool(name="held", bufs=1) as held,
@@ -25,20 +28,21 @@ def tile_lookup_gnorm_relu_kernel(tc, tab, w, b, offs, out):
         lists = held.tile([P, n // 16], U16, name="lists")
         nc.sync.dma_start(lists[:], offs)
 
-        bias = held.tile([P, feature_blocks], F32, name="bias")
-        with nc.allow_non_contiguous_dma(reason="512 bias values, one to a partition and block"):
-            nc.scalar.dma_start(bias[:], b.rearrange("(c p) o -> p (c o)", p=P))
-
         gate_windows = [held.tile([P, places], F32, name=f"gates{k}") for k in range(row_blocks)]
         value_windows = [held.tile([P, places], F32, name=f"values{k}") for k in range(row_blocks)]
-        weights = held.tile([P, row_blocks, features], BF16, name="weights")
         for k in range(row_blocks):
             block = slice(k * P, (k + 1) * P)
             nc.sync.dma_start(gate_windows[k][:], tab[1, block, :])
             nc.sync.dma_start(value_windows[k][:], tab[0, block, :])
-            nc.sync.dma_start(weights[:, k, :], w[block, :])
 
-        sums = [psum.tile([P, n], F32, name=f"sums{c}") for c in range(feature_blocks)]
+        weights = held.tile([P, row_blocks, features], BF16, name="weights")
+        nc.sync.dma_start(weights[:], w.rearrange("(k p) m -> p k m", p=P))
+
+        bias = held.tile([P, per_partition], F32, name="bias")
+        nc.sync.dma_start(bias[:], b.rearrange("(p c) o -> p (c o)", p=P))
+        out_rows = out.rearrange("(p c) n -> p c n", p=P)
+
+        sums = [[psum.tile([P, half], F32, name=f"sums{h}_{c}") for c in range(per_partition)] for h in range(HALVES)]
         for k in range(row_blocks):
             gates = held.tile([P, n], F32, name=f"picked_gates{k}")
             nc.scalar.activation(gates[:], gate_windows[k][:].indirect(lists[:]), ACT.Sigmoid)
@@ -47,20 +51,29 @@ def tile_lookup_gnorm_relu_kernel(tc, tab, w, b, offs, out):
                 values[:], value_windows[k][:].indirect(lists[:]), 0.125, 1.5, ALU.subtract, ALU.mult
             )
             x = held.tile([P, n], BF16, name=f"x{k}")
-            nc.vector.tensor_tensor(x[:], values[:], gates[:], ALU.mult)
-            for c in range(feature_blocks):
-                nc.tensor.matmul(
-                    sums[c][:],
-                    weights[:, k, c * P : (c + 1) * P],
-                    x[:],
-                    start=(k == 0),
-                    stop=(k == row_blocks - 1),
-                )
+            for h in range(HALVES):
+                columns = slice(h * half, (h + 1) * half)
+                nc.vector.tensor_tensor(x[:, columns], values[:, columns], gates[:, columns], ALU.mult)
+            if k == 0:
+                for warm_up in range(WARM_UPS):
+                    nc.tensor.matmul(sums[0][0][:], x[:, 0:P], x[:, 0:half], start=True, stop=True)
+            for h in range(HALVES):
+                columns = slice(h * half, (h + 1) * half)
+                for c in range(per_partition):
+                    nc.tensor.matmul(
+                        sums[h][c][:],
+                        weights[:, k, c::per_partition],
+                        x[:, columns],
+                        start=(k == 0),
+                        stop=(k == row_blocks - 1),
+                    )
 
-        for c in range(feature_blocks):
-            result = held.tile([P, n], F32, name=f"result{c}")
-            if c % 2 == 0:
-                nc.scalar.activation(result[:], sums[c][:], ACT.Relu, bias=bias[:, c : c + 1])
-            else:
-                nc.vector.tensor_scalar(result[:], sums[c][:], bias[:, c : c + 1], 0.0, ALU.add, ALU.max)
-            nc.sync.dma_start(out[c * P : (c + 1) * P, :], result[:])
+        for h in range(HALVES):
+            columns = slice(h * half, (h + 1) * half)
+            for c in range(per_partition):
+                result = held.tile([P, half], F32, name=f"result{h}_{c}")
+                if c % 2 == 0:
+                    nc.scalar.activation(result[:], sums[h][c][:], ACT.Relu, bias=bias[:, c : c + 1])
+                else:
+                    nc.vector.tensor_scalar(result[:], sums[h][c][:], bias[:, c : c + 1], 0.0, ALU.add, ALU.max)
+                nc.sync.dma_start(out_rows[:, c, columns], result[:])

import concourse.mybir as mybir

P = 128
F32 = mybir.dt.float32
BF16 = mybir.dt.bfloat16
U16 = mybir.dt.uint16
ALU = mybir.AluOpType
ACT = mybir.ActivationFunctionType

FLOPS = 2 * 256 * 512 * 512
HALVES = 2
WARM_UPS = 10


def tile_lookup_gnorm_relu_kernel(tc, tab, w, b, offs, out):
    nc = tc.nc
    rows, places = tab.shape[1], tab.shape[2]
    features = w.shape[1]
    n = offs.shape[1] * 16
    row_blocks = rows // P
    per_partition = features // P
    half = n // HALVES

    with (
        tc.tile_pool(name="held", bufs=1) as held,
        tc.psum_pool(name="psum", bufs=1) as psum,
    ):
        lists = held.tile([P, n // 16], U16, name="lists")
        nc.sync.dma_start(lists[:], offs)

        gate_windows = [held.tile([P, places], F32, name=f"gates{k}") for k in range(row_blocks)]
        value_windows = [held.tile([P, places], F32, name=f"values{k}") for k in range(row_blocks)]
        for k in range(row_blocks):
            block = slice(k * P, (k + 1) * P)
            nc.sync.dma_start(gate_windows[k][:], tab[1, block, :])
            nc.sync.dma_start(value_windows[k][:], tab[0, block, :])

        weights = held.tile([P, row_blocks, features], BF16, name="weights")
        nc.sync.dma_start(weights[:], w.rearrange("(k p) m -> p k m", p=P))

        bias = held.tile([P, per_partition], F32, name="bias")
        nc.sync.dma_start(bias[:], b.rearrange("(p c) o -> p (c o)", p=P))
        out_rows = out.rearrange("(p c) n -> p c n", p=P)

        sums = [[psum.tile([P, half], F32, name=f"sums{h}_{c}") for c in range(per_partition)] for h in range(HALVES)]
        for k in range(row_blocks):
            gates = held.tile([P, n], F32, name=f"picked_gates{k}")
            nc.scalar.activation(gates[:], gate_windows[k][:].indirect(lists[:]), ACT.Sigmoid)
            values = held.tile([P, n], F32, name=f"picked_values{k}")
            nc.vector.tensor_scalar(
                values[:], value_windows[k][:].indirect(lists[:]), 0.125, 1.5, ALU.subtract, ALU.mult
            )
            x = held.tile([P, n], BF16, name=f"x{k}")
            for h in range(HALVES):
                columns = slice(h * half, (h + 1) * half)
                nc.vector.tensor_tensor(x[:, columns], values[:, columns], gates[:, columns], ALU.mult)
            if k == 0:
                for warm_up in range(WARM_UPS):
                    nc.tensor.matmul(sums[0][0][:], x[:, 0:P], x[:, 0:half], start=True, stop=True)
            for h in range(HALVES):
                columns = slice(h * half, (h + 1) * half)
                for c in range(per_partition):
                    nc.tensor.matmul(
                        sums[h][c][:],
                        weights[:, k, c::per_partition],
                        x[:, columns],
                        start=(k == 0),
                        stop=(k == row_blocks - 1),
                    )

        for h in range(HALVES):
            columns = slice(h * half, (h + 1) * half)
            for c in range(per_partition):
                result = held.tile([P, half], F32, name=f"result{h}_{c}")
                if c % 2 == 0:
                    nc.scalar.activation(result[:], sums[h][c][:], ACT.Relu, bias=bias[:, c : c + 1])
                else:
                    nc.vector.tensor_scalar(result[:], sums[h][c][:], bias[:, c : c + 1], 0.0, ALU.add, ALU.max)
                nc.sync.dma_start(out_rows[:, c, columns], result[:])
